import numpy as np
import ml_dtypes


def mxq(x, axis, fmt="e4m3"):
    dtype, down = {"e4m3": (ml_dtypes.float8_e4m3fn, 7), "e5m2": (ml_dtypes.float8_e5m2, 14)}[fmt]
    v = np.moveaxis(np.asarray(x, np.float32).astype(ml_dtypes.bfloat16).astype(np.float64), axis, -1)
    blocks = v.reshape(v.shape[:-1] + (-1, 32))
    amax = np.abs(blocks).max(-1, keepdims=True)
    byte = np.maximum(np.where(amax > 0, np.frexp(amax)[1] - 1 + 127, 0) - down, 1)
    scale = np.exp2(byte - 127.0)
    codes = (blocks / scale).astype(np.float32).astype(dtype).astype(np.float64)
    return np.moveaxis((codes * scale).reshape(v.shape), -1, axis)


WIDE = False


def mx_kscale(k):
    if not WIDE:
        return np.ones(k)
    levels = np.array([10, -10, 5, -5, 0])
    if k % 512:
        return np.exp2(np.random.permutation(np.resize(levels, k // 32))).repeat(32)
    a = np.empty((k // 512, 16))
    for p in range(k // 512):
        a[p, :8] = np.random.permutation(np.resize(levels, 8))
        for g in range(8):
            far = levels[np.abs(levels - a[p, g]) >= 10]
            a[p, g + 8] = far[np.random.randint(len(far))]
    return np.exp2(a.ravel()).repeat(32)


def f64(x):
    return np.asarray(x).astype(np.float64)


def striped(idx):
    return np.tile(idx.reshape(-1, 16).T, (8, 1)).astype(np.uint16)


def unstriped(offs):
    return offs[:16].T.reshape(-1).astype(np.int64)


E2M1 = np.array([0.0, 0.5, 1.0, 1.5, 2.0, 3.0, 4.0, 6.0, -0.0, -0.5, -1.0, -1.5, -2.0, -3.0, -4.0, -6.0])


def pack_weight(w, fmt):
    k, n = w.shape
    w = f64(np.asarray(w, np.float32).astype(ml_dtypes.bfloat16)).reshape(k // 32, 32, n)
    amax = np.abs(w).max(1)
    if fmt == "e4m3":
        byte = np.frexp(amax)[1] - 1 + 127 - 7
    else:
        mant, ex = np.frexp(amax / 6.0)
        byte = np.where(mant > 0.5, ex, ex - 1) + 127
    byte = np.clip(np.where(amax > 0, byte, 1), 1, 254)
    scaled = (w * np.exp2(127.0 - byte)[:, None, :]).reshape(k, n).astype(np.float32)
    by_word = np.ascontiguousarray(scaled.reshape(k // 512, 128, 4, n).transpose(0, 1, 3, 2))
    if fmt == "e4m3":
        words = by_word.astype(ml_dtypes.float8_e4m3fn).view(np.uint8)
    else:
        c = by_word.astype(ml_dtypes.float4_e2m1fn).view(np.uint8) & 0xF
        words = (c[..., 0::2] | (c[..., 1::2] << 4)).reshape(k // 512, 128, 2 * n)
    return np.ascontiguousarray(words), np.ascontiguousarray(byte.astype(np.uint8).reshape(k // 512, 16, n))


def unpack_weight(words, scales, fmt):
    g, _, n = scales.shape
    words = np.ascontiguousarray(words).reshape(g, 128, n, -1)
    if fmt == "e4m3":
        vals = words.view(ml_dtypes.float8_e4m3fn).astype(np.float64)
    else:
        nib = np.empty((g, 128, n, 4), np.uint8)
        nib[..., 0::2] = words & 0xF
        nib[..., 1::2] = words >> 4
        vals = E2M1[nib]
    vals = vals * np.repeat(np.exp2(scales.astype(np.float64) - 127.0), 8, axis=1)[..., None]
    return vals.transpose(0, 1, 3, 2).reshape(g * 512, n)


def gelu(v):
    return 0.5 * v * (1.0 + np.tanh(np.sqrt(2.0 / np.pi) * (v + 0.044715 * v**3)))


K, T, S, P, H, N = 1024, 4096, 1024, 512, 1024, 512


def setup_inputs():
    n = np.random.standard_normal
    s = mx_kscale(K)[:, None]
    u = mx_kscale(H)[:, None]
    tab_words, tab_scales = pack_weight(n((K, T)) * s, "e4m3")
    w2_words, w2_scales = pack_weight(n((K, H)) / np.sqrt(K) / s * u.T, "e2m1")
    return {
        "tab_words": tab_words,
        "tab_scales": tab_scales,
        "offs": striped(np.random.permutation(T)[:S]),
        "pos1": striped(np.random.permutation(S)[:P]),
        "pos2": striped(np.random.permutation(S)[:P]),
        "w1": (0.9 * n((K, H)) / np.sqrt(K) / s).astype(np.float32),
        "w2_words": w2_words,
        "w2_scales": w2_scales,
        "corr": (0.8 * n((H, S)) * u).astype(np.float32),
        "slope": np.random.uniform(1, 3, H).astype(np.float32),
        "share": np.random.uniform(0.1, 0.5, H).astype(np.float32),
        "gain": (np.random.uniform(1.5, 4.0, H) * u[:, 0]).astype(np.float32),
        "w3": (1.5 * n((H, N)) / np.sqrt(H) / u).astype(np.float32),
    }


def reference(tab_words, tab_scales, offs, pos1, pos2, w1, w2_words, w2_scales,
              corr, slope, share, gain, w3):
    v = unpack_weight(tab_words, tab_scales, "e4m3")[:, unstriped(offs)]
    w1q = mxq(f64(w1), 0, "e4m3")
    w2 = unpack_weight(w2_words, w2_scales, "e2m1")
    h = w1q.T @ v
    g = (w2.T @ v) + f64(corr)
    top = h.max(axis=1)
    a = 1.0 / (1.0 + np.exp(-f64(slope)[:, None] * (h[:, unstriped(pos1)] - f64(share)[:, None] * top[:, None])))
    c = g[:, unstriped(pos2)]
    z = np.minimum(c, f64(gain)[:, None] * a)
    zq = mxq(z, 0, "e4m3")
    w3q = mxq(f64(w3), 0, "e4m3")
    y = w3q.T @ zq
    return 1.0 / (1.0 + np.square(y))

@@ -1,0 +1,346 @@
+from contextlib import ExitStack
+
+import concourse.mybir as mybir
+
+K, T, S, M, H, N = 1024, 4096, 1024, 512, 1024, 512
+FLOPS = 2 * (2 * K * H * S + H * N * M)
+
+F32 = mybir.dt.float32
+BF16 = mybir.dt.bfloat16
+I32 = mybir.dt.int32
+U32 = mybir.dt.uint32
+U16 = mybir.dt.uint16
+U8 = mybir.dt.uint8
+FP8X4 = mybir.dt.float8_e4m3fn_x4
+FP4X4 = mybir.dt.float4_e2m1fn_x4
+ALU = mybir.AluOpType
+ACT = mybir.ActivationFunctionType
+
+P = 128
+PACK = 4
+PASS = P * PACK
+BANK = 512
+LIST = 16
+PARTS = {0: [(0, 512)], 1: [(0, 256), (256, 512)]}
+OUT_PARTS = PARTS[1]
+
+
+def tile_list_stone_composition_closeness_kernel(
+    tc, tab_words, tab_scales, offs, pos1, pos2, w1, w2_words, w2_scales, corr, slope, share, gain, w3, out
+):
+    nc = tc.nc
+    with ExitStack() as ctx:
+        sb = ctx.enter_context(tc.tile_pool(name="sb", bufs=1))
+        ps = ctx.enter_context(tc.psum_pool(name="ps", bufs=8))
+
+        def tile(shape, dtype, name, tag=None, bufs=1):
+            return sb.tile(shape, dtype, name=name, tag=tag or name, bufs=bufs, align_bytes=64)
+
+        def bank(name):
+            return ps.tile([P, BANK], F32, name=name, tag="bank")
+
+        tab_s = tile([P, 2 * T], U8, "tab_s")
+        nc.vector.memset(tab_s[:, :5120].bitcast(I32), 0)
+        nc.gpsimd.memset(tab_s[:, 5120:].bitcast(I32), 0)
+        w2s_raw = tile([P, 2 * H], U8, "w2s_raw")
+        nc.vector.memset(w2s_raw[:].bitcast(I32), 0)
+
+        offs_t = tile([P, S // LIST], U16, "offs_t")
+        nc.sync.dma_start(offs_t[:], offs)
+        pos1_t = tile([P, M // LIST], U16, "pos1_t")
+        pos2_t = tile([P, M // LIST], U16, "pos2_t")
+        nc.sync.dma_start(pos1_t[:], pos1)
+        nc.sync.dma_start(pos2_t[:], pos2)
+        tab_w = [tile([P, T], I32, "tab_w%d" % a) for a in range(2)]
+
+        def load_tab(a):
+            nc.sync.dma_start(tab_w[a][:], tab_words[a].rearrange("p t i -> p (t i)").bitcast(I32))
+
+        for q in range(4):
+            nc.sync.dma_start(
+                tab_s[32 * q : 32 * q + 4, :].rearrange("r (a t) -> r a t", a=2).bitcast(I32),
+                tab_scales[:, 4 * q : 4 * q + 4, :].rearrange("a r t -> r a t").bitcast(I32),
+            )
+        load_tab(0)
+        for q in range(4):
+            nc.sync.dma_start(
+                w2s_raw[32 * q : 32 * q + 4, :].rearrange("r (a c) -> r a c", a=2).bitcast(I32),
+                w2_scales[:, 4 * q : 4 * q + 4, :].rearrange("a r c -> r a c").bitcast(I32),
+            )
+        load_tab(1)
+
+        w2_raw = [tile([P, 2, PASS], U16, "w2_raw%d" % b) for b in range(2)]
+
+        def load_w2(b):
+            nc.sync.dma_start(
+                w2_raw[b][:].bitcast(I32),
+                w2_words[:, :, 2 * PASS * b : 2 * PASS * (b + 1)].rearrange("a p c -> p a c").bitcast(I32),
+            )
+
+        g = [tile([P, S], F32, "g%d" % s) for s in range(8)]
+        corr_rows = corr.rearrange("(b p i) j -> b i p j", b=2, i=PACK)
+
+        def load_corr(s):
+            nc.sync.dma_start(g[s][:], corr_rows[s // PACK, s % PACK])
+
+        w_raw = {}
+
+        def load_w1(b, a):
+            w_raw[b, a] = tile([P, PACK, PASS], F32, "w1_raw%d%d" % (b, a), tag="w_raw", bufs=4)
+            rows = w1[PASS * a : PASS * (a + 1), PASS * b : PASS * (b + 1)]
+            nc.sync.dma_start(w_raw[b, a][:], rows.rearrange("(p j) c -> p j c", j=PACK))
+
+        w3_raw = {}
+
+        def load_w3(b):
+            w3_raw[b] = tile([P, PACK, N], F32, "w3_raw%d" % b, tag="w_raw", bufs=4)
+            nc.sync.dma_start(w3_raw[b][:], w3[PASS * b : PASS * (b + 1), :].rearrange("(p j) n -> p j n", j=PACK))
+
+        def load_rows(vec, name):
+            t = tile([P, 2, PACK], F32, name)
+            nc.sync.dma_start(t[:], vec.rearrange("(b p i) -> p b i", b=2, i=PACK))
+            return t[:].rearrange("p b i -> p (b i)")
+
+        load_w2(0)
+        load_corr(0)
+        load_corr(1)
+        load_w1(0, 0)
+        load_corr(2)
+        load_w1(0, 1)
+        slope_t = load_rows(slope, "slope_t")
+        share_t = load_rows(share, "share_t")
+        load_corr(3)
+        load_w2(1)
+        load_w1(1, 0)
+        gain_t = load_rows(gain, "gain_t")
+        load_corr(4)
+        load_w1(1, 1)
+        load_corr(5)
+        load_corr(6)
+        load_corr(7)
+
+        v_s = [tile([P, S], U8, "v_s%d" % a) for a in range(2)]
+        for a in range(2):
+            nc.vector.tensor_copy(v_s[a][:], tab_s[:, T * a : T * (a + 1)].indirect(offs_t[:]))
+        v_w = {}
+
+        def gather_words(a):
+            for u in range(2):
+                v_w[a, u] = tile([P, BANK], U32, "v_w%d%d" % (a, u))
+                cols = slice(u * BANK // LIST, (u + 1) * BANK // LIST)
+                nc.vector.tensor_copy(v_w[a, u][:], tab_w[a][:].bitcast(U32).indirect(offs_t[:, cols]))
+
+        gather_words(0)
+        w2_s = tile([P, 2 * H], U8, "w2_s")
+        nc.vector.tensor_copy(
+            w2_s[:].rearrange("p (b i m) -> p b i m", b=4, i=PACK),
+            w2s_raw[:].rearrange("p (b m i) -> p b i m", b=4, i=PACK),
+        )
+        gather_words(1)
+
+        neg_ss = tile([P, 8], F32, "neg_ss")
+        nc.vector.scalar_tensor_tensor(neg_ss[:], slope_t, -1.0, share_t, ALU.mult, ALU.mult)
+
+        w2_w = {}
+
+        def deal_w2(b):
+            w2_w[b] = tile([P, 2, PASS], U16, "w2_w%d" % b)
+            nc.scalar.copy(
+                w2_w[b][:].rearrange("p a (i m) -> p a i m", i=PACK),
+                w2_raw[b][:].rearrange("p a (m i) -> p a i m", i=PACK),
+            )
+
+        def quantize(grouped, name):
+            width = grouped.shape[1] // PACK
+            codes = tile([P, width], U32, name + "_w")
+            scales = tile([P, width], U8, name + "_s")
+            nc.vector.quantize_mx(out=codes[:].bitcast(FP8X4), scales=scales[:], in_=grouped)
+            return codes, scales
+
+        w1_q = {}
+
+        def make_w1(b, a):
+            grouped = tile([P, PASS * PACK], BF16, "w1_bf%d%d" % (b, a), tag="w_bf", bufs=2)
+            dst = grouped[:].rearrange("p (u e m j) -> p u m j e", u=2, e=2, j=PACK)
+            src = w_raw[b, a][:].rearrange("p j (m u e) -> p u m j e", u=2, e=2)
+            for u in range(2):
+                nc.scalar.copy(dst[:, u], src[:, u])
+            w1_q[b, a] = quantize(grouped[:], "w1_q%d%d" % (b, a))
+
+        w3_q = {}
+
+        def make_w3(b):
+            grouped = tile([P, N * PACK], BF16, "w3_bf%d" % b, tag="w_bf", bufs=2)
+            dst = grouped[:].rearrange("p (u c j) -> p u c j", u=4, j=PACK)
+            src = w3_raw[b][:].rearrange("p j (u c) -> p u c j", u=4)
+            for u in range(4):
+                nc.gpsimd.tensor_scalar(dst[:, u], src[:, u], 1.0, 0.0, ALU.mult, ALU.add)
+            w3_q[b] = quantize(grouped[:], "w3_q%d" % b)
+
+        def make_g(s):
+            b, i = divmod(s, PACK)
+            for u in range(2):
+                cols = slice(u * BANK, (u + 1) * BANK)
+                acc = bank("g_acc%d%d" % (s, u))
+                for a in range(2):
+                    nc.tensor.matmul_mx(
+                        out=acc[:],
+                        lhsT=w2_w[b][:, a, P * i : P * (i + 1)].bitcast(FP4X4),
+                        lhsT_scale=w2_s[:, H * a + P * s : H * a + P * (s + 1)],
+                        rhs=v_w[a, u][:].bitcast(FP8X4),
+                        rhs_scale=v_s[a][:, cols],
+                        start=(a == 0),
+                        stop=(a == 1),
+                    )
+                nc.vector.tensor_tensor(g[s][:, cols], acc[:], g[s][:, cols], ALU.add)
+
+        h, bias = {}, {}
+
+        def make_h(s):
+            b, i = divmod(s, PACK)
+            h[s] = tile([P, S], F32, "h%d" % s, tag="h", bufs=4)
+            tops = tile([P, 2], F32, "tops%d" % s)
+            for u in range(2):
+                cols = slice(u * BANK, (u + 1) * BANK)
+                acc = bank("h_acc%d%d" % (s, u))
+                for a in range(2):
+                    codes, scales = w1_q[b, a]
+                    nc.tensor.matmul_mx(
+                        out=acc[:],
+                        lhsT=codes[:, P * i : P * (i + 1)].bitcast(FP8X4),
+                        lhsT_scale=scales[:, P * i : P * (i + 1)],
+                        rhs=v_w[a, u][:].bitcast(FP8X4),
+                        rhs_scale=v_s[a][:, cols],
+                        start=(a == 0),
+                        stop=(a == 1),
+                    )
+                nc.vector.tensor_scalar(
+                    h[s][:, cols], acc[:], 1.0, None, ALU.mult, ALU.max, accum_out=tops[:, u : u + 1]
+                )
+            bias[s] = tile([P, 8], F32, "bias%d" % s)
+            nc.gpsimd.tensor_scalar(
+                bias[s][:, 0:1], tops[:, 0:1], tops[:, 1:2], neg_ss[:, s : s + 1], ALU.max, ALU.mult
+            )
+
+        gate, picked = {}, {}
+
+        def look(s, lo, hi):
+            gate[s, lo] = tile([P, hi - lo], F32, "gate%d_%d" % (s, lo), tag="gate%d" % (hi - lo), bufs=4 * M // (hi - lo))
+            nc.scalar.activation(
+                out=gate[s, lo][:],
+                in_=h[s][:].indirect(pos1_t[:, lo // LIST : hi // LIST]),
+                func=ACT.Sigmoid,
+                bias=bias[s][:, 0:1],
+                scale=slope_t[:, s : s + 1],
+            )
+
+        def pick(s, lo, hi):
+            picked[s, lo] = tile([P, hi - lo], F32, "picked%d_%d" % (s, lo), tag="picked", bufs=5)
+            nc.vector.tensor_copy(picked[s, lo][:], g[s][:].indirect(pos2_t[:, lo // LIST : hi // LIST]))
+
+        z = {}
+
+        def limit(s, lo, hi):
+            b, i = divmod(s, PACK)
+            if i == 0:
+                z[b, lo] = tile([P, PACK, hi - lo], BF16, "z%d_%d" % (b, lo), tag="z", bufs=2)
+            nc.vector.scalar_tensor_tensor(
+                z[b, lo][:, i, :], gate[s, lo][:], gain_t[:, s : s + 1], picked[s, lo][:], ALU.mult, ALU.min
+            )
+
+        z_q = {}
+
+        def make_z(b, lo, hi):
+            grouped = tile([P, (hi - lo) * PACK], BF16, "z_bf%d_%d" % (b, lo), tag="z_bf", bufs=2)
+            dst = grouped[:].rearrange("p (c e j) -> p c j e", e=PACK, j=PACK)
+            src = z[b, lo][:].rearrange("p j (c e) -> p c j e", e=PACK)
+            if lo == 0:
+                nc.scalar.copy(dst, src)
+            else:
+                nc.vector.tensor_copy(dst, src)
+            z_q[b, lo] = quantize(grouped[:], "z_q%d_%d" % (b, lo))
+
+        out_rows = out.rearrange("(t p) m -> p t m", p=P)
+
+        y_acc = {}
+
+        def multiply(b, lo, hi):
+            width = hi - lo
+            per_bank = BANK // width
+            w_codes, w_scales = w3_q[b]
+            if b == 0:
+                z_codes, z_scales = z_q[0, 0][0][:, lo:hi], z_q[0, 0][1][:, lo:hi]
+            else:
+                z_codes, z_scales = z_q[1, lo][0][:], z_q[1, lo][1][:]
+            for t in range(N // P):
+                t0, dt = t - t % per_bank, t % per_bank
+                if b == 0 and dt == 0:
+                    y_acc[lo, t0] = bank("y_acc%d_%d" % (lo, t0))
+                nc.tensor.matmul_mx(
+                    out=y_acc[lo, t0][:, dt * width : (dt + 1) * width],
+                    lhsT=w_codes[:, P * t : P * (t + 1)].bitcast(FP8X4),
+                    lhsT_scale=w_scales[:, P * t : P * (t + 1)],
+                    rhs=z_codes.bitcast(FP8X4),
+                    rhs_scale=z_scales,
+                    start=(b == 0 and dt == 0),
+                    stop=(b == 1 and dt == per_bank - 1),
+                )
+
+        def finish(lo, hi):
+            per_bank = BANK // (hi - lo)
+            for t0 in range(0, N // P, per_bank):
+                square = tile([P, BANK], F32, "square%d_%d" % (lo, t0), tag="square", bufs=2)
+                nc.scalar.activation(out=square[:], in_=y_acc[lo, t0][:], func=ACT.Square)
+                root = tile([P, BANK], F32, "root%d_%d" % (lo, t0), tag="root", bufs=2)
+                nc.scalar.activation(out=root[:], in_=square[:], func=ACT.Abs_reciprocal_sqrt, bias=1.0)
+                close = tile([P, BANK], F32, "close%d_%d" % (lo, t0), tag="close", bufs=4)
+                if lo == 0:
+                    nc.scalar.activation(out=close[:], in_=root[:], func=ACT.Square)
+                else:
+                    nc.vector.tensor_tensor(close[:], root[:], root[:], ALU.mult)
+                nc.sync.dma_start(
+                    out_rows[:, t0 : t0 + per_bank, lo:hi], close[:].rearrange("p (t m) -> p t m", t=per_bank)
+                )
+
+        deal_w2(0)
+        make_g(0)
+        make_g(1)
+        pick(0, 0, M)
+        pick(1, 0, M)
+        make_w1(0, 0)
+        make_g(2)
+        pick(2, 0, M)
+        make_w1(0, 1)
+        load_w3(0)
+        load_w3(1)
+        deal_w2(1)
+        for s in range(4):
+            make_h(s)
+            look(s, 0, M)
+        make_g(3)
+        pick(3, 0, M)
+        make_w1(1, 0)
+        make_w1(1, 1)
+        for s in range(4):
+            limit(s, 0, M)
+        for s in range(4, 8):
+            make_h(s)
+            look(s, *PARTS[1][0])
+        make_z(0, 0, M)
+        for s in range(4, 8):
+            make_g(s)
+        for s in range(4, 8):
+            look(s, *PARTS[1][1])
+        make_w3(0)
+        make_w3(1)
+        for lo, hi in PARTS[1]:
+            multiply(0, lo, hi)
+        for lo, hi in PARTS[1]:
+            for s in range(4, 8):
+                pick(s, lo, hi)
+            for s in range(4, 8):
+                limit(s, lo, hi)
+            make_z(1, lo, hi)
+        for lo, hi in OUT_PARTS:
+            multiply(1, lo, hi)
+            finish(lo, hi)

@@ -21,8 +21,7 @@ PACK = 4
 PASS = P * PACK
 BANK = 512
 LIST = 16
-PARTS = {0: [(0, 512)], 1: [(0, 256), (256, 512)]}
-OUT_PARTS = PARTS[1]
+HALF = M // 2
 
 
 def tile_list_stone_composition_closeness_kernel(
@@ -103,21 +102,17 @@ def tile_list_stone_composition_closeness_kernel(
 
         load_w2(0)
         load_corr(0)
-        load_corr(1)
         load_w1(0, 0)
-        load_corr(2)
+        load_corr(1)
         load_w1(0, 1)
+        load_corr(2)
         slope_t = load_rows(slope, "slope_t")
         share_t = load_rows(share, "share_t")
-        load_corr(3)
         load_w2(1)
         load_w1(1, 0)
-        gain_t = load_rows(gain, "gain_t")
-        load_corr(4)
+        load_corr(3)
         load_w1(1, 1)
-        load_corr(5)
-        load_corr(6)
-        load_corr(7)
+        gain_t = load_rows(gain, "gain_t")
 
         v_s = [tile([P, S], U8, "v_s%d" % a) for a in range(2)]
         for a in range(2):
@@ -171,10 +166,10 @@ def tile_list_stone_composition_closeness_kernel(
 
         def make_w3(b):
             grouped = tile([P, N * PACK], BF16, "w3_bf%d" % b, tag="w_bf", bufs=2)
-            dst = grouped[:].rearrange("p (u c j) -> p u c j", u=4, j=PACK)
-            src = w3_raw[b][:].rearrange("p j (u c) -> p u c j", u=4)
-            for u in range(4):
-                nc.gpsimd.tensor_scalar(dst[:, u], src[:, u], 1.0, 0.0, ALU.mult, ALU.add)
+            dst = grouped[:].rearrange("p (u c e j) -> p u c j e", u=2, e=PACK, j=PACK)
+            src = w3_raw[b][:].rearrange("p j (u c e) -> p u c j e", u=2, e=PACK)
+            for u in range(2):
+                nc.scalar.copy(dst[:, u], src[:, u])
             w3_q[b] = quantize(grouped[:], "w3_q%d" % b)
 
         def make_g(s):
@@ -218,129 +213,144 @@ def tile_list_stone_composition_closeness_kernel(
                     h[s][:, cols], acc[:], 1.0, None, ALU.mult, ALU.max, accum_out=tops[:, u : u + 1]
                 )
             bias[s] = tile([P, 8], F32, "bias%d" % s)
-            nc.gpsimd.tensor_scalar(
+            nc.vector.tensor_scalar(
                 bias[s][:, 0:1], tops[:, 0:1], tops[:, 1:2], neg_ss[:, s : s + 1], ALU.max, ALU.mult
             )
 
-        gate, picked = {}, {}
+        gate = {}
 
-        def look(s, lo, hi):
-            gate[s, lo] = tile([P, hi - lo], F32, "gate%d_%d" % (s, lo), tag="gate%d" % (hi - lo), bufs=4 * M // (hi - lo))
+        def look(s):
+            gate[s] = tile([P, M], F32, "gate%d" % s)
             nc.scalar.activation(
-                out=gate[s, lo][:],
-                in_=h[s][:].indirect(pos1_t[:, lo // LIST : hi // LIST]),
+                out=gate[s][:],
+                in_=h[s][:].indirect(pos1_t[:]),
                 func=ACT.Sigmoid,
                 bias=bias[s][:, 0:1],
                 scale=slope_t[:, s : s + 1],
             )
 
-        def pick(s, lo, hi):
-            picked[s, lo] = tile([P, hi - lo], F32, "picked%d_%d" % (s, lo), tag="picked", bufs=5)
-            nc.vector.tensor_copy(picked[s, lo][:], g[s][:].indirect(pos2_t[:, lo // LIST : hi // LIST]))
+        picked = {}
 
-        z = {}
+        def pick_whole(s):
+            whole = tile([P, M], F32, "picked%d" % s)
+            nc.vector.tensor_copy(whole[:], g[s][:].indirect(pos2_t[:]))
+            for part in range(2):
+                picked[s, part] = whole[:, HALF * part : HALF * (part + 1)]
 
-        def limit(s, lo, hi):
-            b, i = divmod(s, PACK)
-            if i == 0:
-                z[b, lo] = tile([P, PACK, hi - lo], BF16, "z%d_%d" % (b, lo), tag="z", bufs=2)
+        def pick_half(s, part, into):
+            cols = slice(part * HALF // LIST, (part + 1) * HALF // LIST)
+            picked[s, part] = into[:, s % PACK, :]
+            nc.vector.tensor_copy(picked[s, part], g[s][:].indirect(pos2_t[:, cols]))
+
+        def limit(s, part, z_rows):
             nc.vector.scalar_tensor_tensor(
-                z[b, lo][:, i, :], gate[s, lo][:], gain_t[:, s : s + 1], picked[s, lo][:], ALU.mult, ALU.min
+                z_rows[:, s % PACK, :],
+                gate[s][:, HALF * part : HALF * (part + 1)],
+                gain_t[:, s : s + 1],
+                picked[s, part],
+                ALU.mult,
+                ALU.min,
             )
 
         z_q = {}
 
-        def make_z(b, lo, hi):
-            grouped = tile([P, (hi - lo) * PACK], BF16, "z_bf%d_%d" % (b, lo), tag="z_bf", bufs=2)
+        def make_z(b, part, z_rows):
+            grouped = tile([P, HALF * PACK], BF16, "z_bf%d_%d" % (b, part), tag="z_bf", bufs=2)
             dst = grouped[:].rearrange("p (c e j) -> p c j e", e=PACK, j=PACK)
-            src = z[b, lo][:].rearrange("p j (c e) -> p c j e", e=PACK)
-            if lo == 0:
+            src = z_rows.rearrange("p j (c e) -> p c j e", e=PACK)
+            if part == 0:
                 nc.scalar.copy(dst, src)
             else:
                 nc.vector.tensor_copy(dst, src)
-            z_q[b, lo] = quantize(grouped[:], "z_q%d_%d" % (b, lo))
+            z_q[b, part] = quantize(grouped[:], "z_q%d_%d" % (b, part))
 
         out_rows = out.rearrange("(t p) m -> p t m", p=P)
 
         y_acc = {}
 
-        def multiply(b, lo, hi):
-            width = hi - lo
-            per_bank = BANK // width
+        def multiply(b, part):
             w_codes, w_scales = w3_q[b]
-            if b == 0:
-                z_codes, z_scales = z_q[0, 0][0][:, lo:hi], z_q[0, 0][1][:, lo:hi]
-            else:
-                z_codes, z_scales = z_q[1, lo][0][:], z_q[1, lo][1][:]
+            z_codes, z_scales = z_q[b, part]
             for t in range(N // P):
-                t0, dt = t - t % per_bank, t % per_bank
+                pair, dt = divmod(t, 2)
                 if b == 0 and dt == 0:
-                    y_acc[lo, t0] = bank("y_acc%d_%d" % (lo, t0))
+                    y_acc[part, pair] = bank("y_acc%d_%d" % (part, pair))
                 nc.tensor.matmul_mx(
-                    out=y_acc[lo, t0][:, dt * width : (dt + 1) * width],
+                    out=y_acc[part, pair][:, dt * HALF : (dt + 1) * HALF],
                     lhsT=w_codes[:, P * t : P * (t + 1)].bitcast(FP8X4),
                     lhsT_scale=w_scales[:, P * t : P * (t + 1)],
-                    rhs=z_codes.bitcast(FP8X4),
-                    rhs_scale=z_scales,
+                    rhs=z_codes[:].bitcast(FP8X4),
+                    rhs_scale=z_scales[:],
                     start=(b == 0 and dt == 0),
-                    stop=(b == 1 and dt == per_bank - 1),
+                    stop=(b == 1 and dt == 1),
                 )
 
-        def finish(lo, hi):
-            per_bank = BANK // (hi - lo)
-            for t0 in range(0, N // P, per_bank):
-                square = tile([P, BANK], F32, "square%d_%d" % (lo, t0), tag="square", bufs=2)
-                nc.scalar.activation(out=square[:], in_=y_acc[lo, t0][:], func=ACT.Square)
-                root = tile([P, BANK], F32, "root%d_%d" % (lo, t0), tag="root", bufs=2)
+        def finish(part):
+            for pair in range(2):
+                square = tile([P, BANK], F32, "square%d_%d" % (part, pair), tag="square", bufs=2)
+                nc.scalar.activation(out=square[:], in_=y_acc[part, pair][:], func=ACT.Square)
+                root = tile([P, BANK], F32, "root%d_%d" % (part, pair), tag="root", bufs=2)
                 nc.scalar.activation(out=root[:], in_=square[:], func=ACT.Abs_reciprocal_sqrt, bias=1.0)
-                close = tile([P, BANK], F32, "close%d_%d" % (lo, t0), tag="close", bufs=4)
-                if lo == 0:
+                close = tile([P, BANK], F32, "close%d_%d" % (part, pair), tag="close", bufs=4)
+                if part == 0:
                     nc.scalar.activation(out=close[:], in_=root[:], func=ACT.Square)
                 else:
                     nc.vector.tensor_tensor(close[:], root[:], root[:], ALU.mult)
                 nc.sync.dma_start(
-                    out_rows[:, t0 : t0 + per_bank, lo:hi], close[:].rearrange("p (t m) -> p t m", t=per_bank)
+                    out_rows[:, 2 * pair : 2 * pair + 2, HALF * part : HALF * (part + 1)],
+                    close[:].rearrange("p (t m) -> p t m", t=2),
                 )
 
         deal_w2(0)
         make_g(0)
-        make_g(1)
-        pick(0, 0, M)
-        pick(1, 0, M)
+        pick_whole(0)
         make_w1(0, 0)
-        make_g(2)
-        pick(2, 0, M)
+        make_g(1)
+        pick_whole(1)
         make_w1(0, 1)
         load_w3(0)
+        load_corr(4)
         load_w3(1)
+        load_corr(5)
+        load_corr(6)
+        load_corr(7)
+        make_g(2)
+        pick_whole(2)
         deal_w2(1)
+        make_w1(1, 0)
         for s in range(4):
             make_h(s)
-            look(s, 0, M)
-        make_g(3)
-        pick(3, 0, M)
-        make_w1(1, 0)
+            look(s)
         make_w1(1, 1)
+        make_g(3)
+        pick_whole(3)
+        z_first = tile([P, PACK, HALF], BF16, "z_first")
         for s in range(4):
-            limit(s, 0, M)
+            limit(s, 0, z_first)
         for s in range(4, 8):
             make_h(s)
-            look(s, *PARTS[1][0])
-        make_z(0, 0, M)
+            look(s)
+        make_w3(0)
+        make_z(0, 0, z_first[:])
+        make_w3(1)
+        multiply(0, 0)
+        left = tile([P, PACK, HALF], F32, "left", tag="picked_half")
+        z_left = tile([P, PACK, HALF], BF16, "z_left", tag="z_late")
         for s in range(4, 8):
             make_g(s)
+            pick_half(s, 0, left)
+            limit(s, 0, z_left)
+        make_z(1, 0, z_left[:])
+        multiply(1, 0)
+        right = tile([P, PACK, HALF], F32, "right", tag="picked_half")
         for s in range(4, 8):
-            look(s, *PARTS[1][1])
-        make_w3(0)
-        make_w3(1)
-        for lo, hi in PARTS[1]:
-            multiply(0, lo, hi)
-        for lo, hi in PARTS[1]:
-            for s in range(4, 8):
-                pick(s, lo, hi)
-            for s in range(4, 8):
-                limit(s, lo, hi)
-            make_z(1, lo, hi)
-        for lo, hi in OUT_PARTS:
-            multiply(1, lo, hi)
-            finish(lo, hi)
+            pick_half(s, 1, right)
+        z_right = tile([P, 2, PACK, HALF], BF16, "z_right", tag="z_late")
+        for b in range(2):
+            for s in range(PACK * b, PACK * (b + 1)):
+                limit(s, 1, z_right[:, b])
+            make_z(b, 1, z_right[:, b])
+        finish(0)
+        for b in range(2):
+            multiply(b, 1)
+        finish(1)

@@ -38,34 +38,33 @@ def tile_list_stone_composition_closeness_kernel(
         def bank(name):
             return ps.tile([P, BANK], F32, name=name, tag="bank")
 
-        tab_s = tile([P, 2 * T], U8, "tab_s")
-        nc.vector.memset(tab_s[:, :5120].bitcast(I32), 0)
-        nc.gpsimd.memset(tab_s[:, 5120:].bitcast(I32), 0)
         w2s_raw = tile([P, 2 * H], U8, "w2s_raw")
         nc.vector.memset(w2s_raw[:].bitcast(I32), 0)
+        tab_s = tile([P, 2 * T], U8, "tab_s")
+        nc.vector.memset(tab_s[:, :T].bitcast(I32), 0)
+        nc.gpsimd.memset(tab_s[:, T:].bitcast(I32), 0)
 
         offs_t = tile([P, S // LIST], U16, "offs_t")
         nc.sync.dma_start(offs_t[:], offs)
-        pos1_t = tile([P, M // LIST], U16, "pos1_t")
-        pos2_t = tile([P, M // LIST], U16, "pos2_t")
-        nc.sync.dma_start(pos1_t[:], pos1)
-        nc.sync.dma_start(pos2_t[:], pos2)
         tab_w = [tile([P, T], I32, "tab_w%d" % a) for a in range(2)]
 
         def load_tab(a):
             nc.sync.dma_start(tab_w[a][:], tab_words[a].rearrange("p t i -> p (t i)").bitcast(I32))
 
-        for q in range(4):
-            nc.sync.dma_start(
-                tab_s[32 * q : 32 * q + 4, :].rearrange("r (a t) -> r a t", a=2).bitcast(I32),
-                tab_scales[:, 4 * q : 4 * q + 4, :].rearrange("a r t -> r a t").bitcast(I32),
-            )
+        def load_scale_rows(plane, scales):
+            rows = scales.rearrange("a (q r) c -> r q a c", r=4)
+            for r in range(4):
+                nc.sync.dma_start(
+                    plane[r:P:32, :].rearrange("q (a c) -> q a c", a=2).bitcast(I32), rows[r].bitcast(I32)
+                )
+
         load_tab(0)
-        for q in range(4):
-            nc.sync.dma_start(
-                w2s_raw[32 * q : 32 * q + 4, :].rearrange("r (a c) -> r a c", a=2).bitcast(I32),
-                w2_scales[:, 4 * q : 4 * q + 4, :].rearrange("a r c -> r a c").bitcast(I32),
-            )
+        pos1_t = tile([P, M // LIST], U16, "pos1_t")
+        pos2_t = tile([P, M // LIST], U16, "pos2_t")
+        nc.sync.dma_start(pos1_t[:], pos1)
+        nc.sync.dma_start(pos2_t[:], pos2)
+        load_scale_rows(w2s_raw, w2_scales)
+        load_scale_rows(tab_s, tab_scales)
         load_tab(1)
 
         w2_raw = [tile([P, 2, PASS], U16, "w2_raw%d" % b) for b in range(2)]
@@ -114,9 +113,6 @@ def tile_list_stone_composition_closeness_kernel(
         load_w1(1, 1)
         gain_t = load_rows(gain, "gain_t")
 
-        v_s = [tile([P, S], U8, "v_s%d" % a) for a in range(2)]
-        for a in range(2):
-            nc.vector.tensor_copy(v_s[a][:], tab_s[:, T * a : T * (a + 1)].indirect(offs_t[:]))
         v_w = {}
 
         def gather_words(a):
@@ -125,12 +121,20 @@ def tile_list_stone_composition_closeness_kernel(
                 cols = slice(u * BANK // LIST, (u + 1) * BANK // LIST)
                 nc.vector.tensor_copy(v_w[a, u][:], tab_w[a][:].bitcast(U32).indirect(offs_t[:, cols]))
 
+        w2_s = {}
+
+        def deal_w2_scales(b):
+            w2_s[b] = tile([P, 2, PASS], U8, "w2_s%d" % b)
+            nc.vector.tensor_copy(
+                w2_s[b][:].rearrange("p a (i m) -> p a i m", i=PACK),
+                w2s_raw[:].rearrange("p (a b m i) -> p b a i m", a=2, b=2, i=PACK)[:, b],
+            )
+
         gather_words(0)
-        w2_s = tile([P, 2 * H], U8, "w2_s")
-        nc.vector.tensor_copy(
-            w2_s[:].rearrange("p (b i m) -> p b i m", b=4, i=PACK),
-            w2s_raw[:].rearrange("p (b m i) -> p b i m", b=4, i=PACK),
-        )
+        deal_w2_scales(0)
+        v_s = [tile([P, S], U8, "v_s%d" % a) for a in range(2)]
+        for a in range(2):
+            nc.vector.tensor_copy(v_s[a][:], tab_s[:, T * a : T * (a + 1)].indirect(offs_t[:]))
         gather_words(1)
 
         neg_ss = tile([P, 8], F32, "neg_ss")
@@ -181,7 +185,7 @@ def tile_list_stone_composition_closeness_kernel(
                     nc.tensor.matmul_mx(
                         out=acc[:],
                         lhsT=w2_w[b][:, a, P * i : P * (i + 1)].bitcast(FP4X4),
-                        lhsT_scale=w2_s[:, H * a + P * s : H * a + P * (s + 1)],
+                        lhsT_scale=w2_s[b][:, a, P * i : P * (i + 1)],
                         rhs=v_w[a, u][:].bitcast(FP8X4),
                         rhs_scale=v_s[a][:, cols],
                         start=(a == 0),
@@ -213,7 +217,7 @@ def tile_list_stone_composition_closeness_kernel(
                     h[s][:, cols], acc[:], 1.0, None, ALU.mult, ALU.max, accum_out=tops[:, u : u + 1]
                 )
             bias[s] = tile([P, 8], F32, "bias%d" % s)
-            nc.vector.tensor_scalar(
+            nc.gpsimd.tensor_scalar(
                 bias[s][:, 0:1], tops[:, 0:1], tops[:, 1:2], neg_ss[:, s : s + 1], ALU.max, ALU.mult
             )
 
@@ -288,7 +292,12 @@ def tile_list_stone_composition_closeness_kernel(
         def finish(part):
             for pair in range(2):
                 square = tile([P, BANK], F32, "square%d_%d" % (part, pair), tag="square", bufs=2)
-                nc.scalar.activation(out=square[:], in_=y_acc[part, pair][:], func=ACT.Square)
+                if (part, pair) == (1, 1):
+                    y_copy = tile([P, BANK], F32, "y_copy")
+                    nc.vector.tensor_copy(y_copy[:], y_acc[part, pair][:])
+                    nc.vector.tensor_tensor(square[:], y_acc[part, pair][:], y_copy[:], ALU.mult)
+                else:
+                    nc.scalar.activation(out=square[:], in_=y_acc[part, pair][:], func=ACT.Square)
                 root = tile([P, BANK], F32, "root%d_%d" % (part, pair), tag="root", bufs=2)
                 nc.scalar.activation(out=root[:], in_=square[:], func=ACT.Abs_reciprocal_sqrt, bias=1.0)
                 close = tile([P, BANK], F32, "close%d_%d" % (part, pair), tag="close", bufs=4)
@@ -304,6 +313,7 @@ def tile_list_stone_composition_closeness_kernel(
         deal_w2(0)
         make_g(0)
         pick_whole(0)
+        deal_w2_scales(1)
         make_w1(0, 0)
         make_g(1)
         pick_whole(1)

@@ -21,7 +21,10 @@ PACK = 4
 PASS = P * PACK
 BANK = 512
 LIST = 16
-HALF = M // 2
+PARTS = ((0, 128), (128, 256), (384, 128))
+CLEAR = 5120
+BANKS = {"g": 4, "h": 4}
+SHARED = ()
 
 
 def tile_list_stone_composition_closeness_kernel(
@@ -30,22 +33,26 @@ def tile_list_stone_composition_closeness_kernel(
     nc = tc.nc
     with ExitStack() as ctx:
         sb = ctx.enter_context(tc.tile_pool(name="sb", bufs=1))
-        ps = ctx.enter_context(tc.psum_pool(name="ps", bufs=8))
+        ps = ctx.enter_context(tc.psum_pool(name="ps", bufs=1))
 
         def tile(shape, dtype, name, tag=None, bufs=1):
             return sb.tile(shape, dtype, name=name, tag=tag or name, bufs=bufs, align_bytes=64)
 
-        def bank(name):
-            return ps.tile([P, BANK], F32, name=name, tag="bank")
+        def bank(name, tag):
+            return ps.tile([P, BANK], F32, name=name, tag=tag, bufs=BANKS[tag])
 
+        tab_s = tile([P, 2 * T], U8, "tab_s")
+        nc.vector.memset(tab_s[:, :CLEAR].bitcast(I32), 0)
+        nc.gpsimd.memset(tab_s[:, CLEAR:].bitcast(I32), 0)
         w2s_raw = tile([P, 2 * H], U8, "w2s_raw")
         nc.vector.memset(w2s_raw[:].bitcast(I32), 0)
-        tab_s = tile([P, 2 * T], U8, "tab_s")
-        nc.vector.memset(tab_s[:, :T].bitcast(I32), 0)
-        nc.gpsimd.memset(tab_s[:, T:].bitcast(I32), 0)
 
         offs_t = tile([P, S // LIST], U16, "offs_t")
         nc.sync.dma_start(offs_t[:], offs)
+        pos1_t = tile([P, M // LIST], U16, "pos1_t")
+        pos2_t = tile([P, M // LIST], U16, "pos2_t")
+        nc.sync.dma_start(pos1_t[:], pos1)
+        nc.sync.dma_start(pos2_t[:], pos2)
         tab_w = [tile([P, T], I32, "tab_w%d" % a) for a in range(2)]
 
         def load_tab(a):
@@ -57,15 +64,6 @@ def tile_list_stone_composition_closeness_kernel(
                 nc.sync.dma_start(
                     plane[r:P:32, :].rearrange("q (a c) -> q a c", a=2).bitcast(I32), rows[r].bitcast(I32)
                 )
-
-        load_tab(0)
-        pos1_t = tile([P, M // LIST], U16, "pos1_t")
-        pos2_t = tile([P, M // LIST], U16, "pos2_t")
-        nc.sync.dma_start(pos1_t[:], pos1)
-        nc.sync.dma_start(pos2_t[:], pos2)
-        load_scale_rows(w2s_raw, w2_scales)
-        load_scale_rows(tab_s, tab_scales)
-        load_tab(1)
 
         w2_raw = [tile([P, 2, PASS], U16, "w2_raw%d" % b) for b in range(2)]
 
@@ -100,6 +98,10 @@ def tile_list_stone_composition_closeness_kernel(
             return t[:].rearrange("p b i -> p (b i)")
 
         load_w2(0)
+        load_scale_rows(tab_s, tab_scales)
+        load_tab(0)
+        load_scale_rows(w2s_raw, w2_scales)
+        load_tab(1)
         load_corr(0)
         load_w1(0, 0)
         load_corr(1)
@@ -109,8 +111,8 @@ def tile_list_stone_composition_closeness_kernel(
         share_t = load_rows(share, "share_t")
         load_w2(1)
         load_w1(1, 0)
-        load_corr(3)
         load_w1(1, 1)
+        load_corr(3)
         gain_t = load_rows(gain, "gain_t")
 
         v_w = {}
@@ -130,12 +132,13 @@ def tile_list_stone_composition_closeness_kernel(
                 w2s_raw[:].rearrange("p (a b m i) -> p b a i m", a=2, b=2, i=PACK)[:, b],
             )
 
-        gather_words(0)
-        deal_w2_scales(0)
         v_s = [tile([P, S], U8, "v_s%d" % a) for a in range(2)]
         for a in range(2):
             nc.vector.tensor_copy(v_s[a][:], tab_s[:, T * a : T * (a + 1)].indirect(offs_t[:]))
+        gather_words(0)
+        deal_w2_scales(0)
         gather_words(1)
+        deal_w2_scales(1)
 
         neg_ss = tile([P, 8], F32, "neg_ss")
         nc.vector.scalar_tensor_tensor(neg_ss[:], slope_t, -1.0, share_t, ALU.mult, ALU.mult)
@@ -159,28 +162,28 @@ def tile_list_stone_composition_closeness_kernel(
         w1_q = {}
 
         def make_w1(b, a):
-            grouped = tile([P, PASS * PACK], BF16, "w1_bf%d%d" % (b, a), tag="w_bf", bufs=2)
+            name = "w1_bf%d%d" % (b, a)
+            grouped = tile([P, PASS * PACK], BF16, name, tag="w_bf", bufs=2)
             dst = grouped[:].rearrange("p (u e m j) -> p u m j e", u=2, e=2, j=PACK)
             src = w_raw[b, a][:].rearrange("p j (m u e) -> p u m j e", u=2, e=2)
             for u in range(2):
                 nc.scalar.copy(dst[:, u], src[:, u])
             w1_q[b, a] = quantize(grouped[:], "w1_q%d%d" % (b, a))
 
-        w3_q = {}
+        w3_bf, w3_q = {}, {}
 
-        def make_w3(b):
-            grouped = tile([P, N * PACK], BF16, "w3_bf%d" % b, tag="w_bf", bufs=2)
-            dst = grouped[:].rearrange("p (u c e j) -> p u c j e", u=2, e=PACK, j=PACK)
+        def round_w3(b):
+            w3_bf[b] = tile([P, N * PACK], BF16, "w3_bf%d" % b, tag="w_bf", bufs=2)
+            dst = w3_bf[b][:].rearrange("p (u c e j) -> p u c j e", u=2, e=PACK, j=PACK)
             src = w3_raw[b][:].rearrange("p j (u c e) -> p u c j e", u=2, e=PACK)
             for u in range(2):
                 nc.scalar.copy(dst[:, u], src[:, u])
-            w3_q[b] = quantize(grouped[:], "w3_q%d" % b)
 
         def make_g(s):
             b, i = divmod(s, PACK)
             for u in range(2):
                 cols = slice(u * BANK, (u + 1) * BANK)
-                acc = bank("g_acc%d%d" % (s, u))
+                acc = bank("g_acc%d%d" % (s, u), "g")
                 for a in range(2):
                     nc.tensor.matmul_mx(
                         out=acc[:],
@@ -191,7 +194,12 @@ def tile_list_stone_composition_closeness_kernel(
                         start=(a == 0),
                         stop=(a == 1),
                     )
-                nc.vector.tensor_tensor(g[s][:, cols], acc[:], g[s][:, cols], ALU.add)
+                if s in SHARED:
+                    sums = tile([P, BANK], F32, "sums%d%d" % (s, u), tag="sums", bufs=3)
+                    nc.scalar.copy(sums[:], acc[:])
+                    nc.gpsimd.tensor_tensor(g[s][:, cols], sums[:], g[s][:, cols], ALU.add)
+                else:
+                    nc.vector.tensor_tensor(g[s][:, cols], acc[:], g[s][:, cols], ALU.add)
 
         h, bias = {}, {}
 
@@ -201,7 +209,7 @@ def tile_list_stone_composition_closeness_kernel(
             tops = tile([P, 2], F32, "tops%d" % s)
             for u in range(2):
                 cols = slice(u * BANK, (u + 1) * BANK)
-                acc = bank("h_acc%d%d" % (s, u))
+                acc = bank("h_acc%d%d" % (s, u), "h")
                 for a in range(2):
                     codes, scales = w1_q[b, a]
                     nc.tensor.matmul_mx(
@@ -233,134 +241,120 @@ def tile_list_stone_composition_closeness_kernel(
                 scale=slope_t[:, s : s + 1],
             )
 
-        picked = {}
+        def pick(s, lo, into):
+            cols = slice(lo // LIST, (lo + into.shape[1]) // LIST)
+            nc.vector.tensor_copy(into, g[s][:].indirect(pos2_t[:, cols]))
 
-        def pick_whole(s):
-            whole = tile([P, M], F32, "picked%d" % s)
-            nc.vector.tensor_copy(whole[:], g[s][:].indirect(pos2_t[:]))
-            for part in range(2):
-                picked[s, part] = whole[:, HALF * part : HALF * (part + 1)]
-
-        def pick_half(s, part, into):
-            cols = slice(part * HALF // LIST, (part + 1) * HALF // LIST)
-            picked[s, part] = into[:, s % PACK, :]
-            nc.vector.tensor_copy(picked[s, part], g[s][:].indirect(pos2_t[:, cols]))
-
-        def limit(s, part, z_rows):
+        def limit(s, lo, picked, z_row):
+            width = picked.shape[1]
             nc.vector.scalar_tensor_tensor(
-                z_rows[:, s % PACK, :],
-                gate[s][:, HALF * part : HALF * (part + 1)],
-                gain_t[:, s : s + 1],
-                picked[s, part],
-                ALU.mult,
-                ALU.min,
+                z_row, gate[s][:, lo : lo + width], gain_t[:, s : s + 1], picked, ALU.mult, ALU.min
             )
 
-        z_q = {}
-
-        def make_z(b, part, z_rows):
-            grouped = tile([P, HALF * PACK], BF16, "z_bf%d_%d" % (b, part), tag="z_bf", bufs=2)
-            dst = grouped[:].rearrange("p (c e j) -> p c j e", e=PACK, j=PACK)
+        def weave(grouped, z_rows, on_scalar):
+            dst = grouped.rearrange("p (c e j) -> p c j e", e=PACK, j=PACK)
             src = z_rows.rearrange("p j (c e) -> p c j e", e=PACK)
-            if part == 0:
+            if on_scalar:
                 nc.scalar.copy(dst, src)
             else:
                 nc.vector.tensor_copy(dst, src)
-            z_q[b, part] = quantize(grouped[:], "z_q%d_%d" % (b, part))
 
         out_rows = out.rearrange("(t p) m -> p t m", p=P)
-
         y_acc = {}
 
-        def multiply(b, part):
+        def multiply(b, part, z_codes, z_scales):
+            width = PARTS[part][1]
+            per_bank = BANK // width
             w_codes, w_scales = w3_q[b]
-            z_codes, z_scales = z_q[b, part]
             for t in range(N // P):
-                pair, dt = divmod(t, 2)
+                k, dt = divmod(t, per_bank)
                 if b == 0 and dt == 0:
-                    y_acc[part, pair] = bank("y_acc%d_%d" % (part, pair))
+                    y_acc[part, k] = bank("y_acc%d_%d" % (part, k), "h")
                 nc.tensor.matmul_mx(
-                    out=y_acc[part, pair][:, dt * HALF : (dt + 1) * HALF],
+                    out=y_acc[part, k][:, dt * width : (dt + 1) * width],
                     lhsT=w_codes[:, P * t : P * (t + 1)].bitcast(FP8X4),
                     lhsT_scale=w_scales[:, P * t : P * (t + 1)],
-                    rhs=z_codes[:].bitcast(FP8X4),
-                    rhs_scale=z_scales[:],
+                    rhs=z_codes.bitcast(FP8X4),
+                    rhs_scale=z_scales,
                     start=(b == 0 and dt == 0),
-                    stop=(b == 1 and dt == 1),
+                    stop=(b == 1 and dt == per_bank - 1),
                 )
 
-        def finish(part):
-            for pair in range(2):
-                square = tile([P, BANK], F32, "square%d_%d" % (part, pair), tag="square", bufs=2)
-                if (part, pair) == (1, 1):
-                    y_copy = tile([P, BANK], F32, "y_copy")
-                    nc.vector.tensor_copy(y_copy[:], y_acc[part, pair][:])
-                    nc.vector.tensor_tensor(square[:], y_acc[part, pair][:], y_copy[:], ALU.mult)
-                else:
-                    nc.scalar.activation(out=square[:], in_=y_acc[part, pair][:], func=ACT.Square)
-                root = tile([P, BANK], F32, "root%d_%d" % (part, pair), tag="root", bufs=2)
-                nc.scalar.activation(out=root[:], in_=square[:], func=ACT.Abs_reciprocal_sqrt, bias=1.0)
-                close = tile([P, BANK], F32, "close%d_%d" % (part, pair), tag="close", bufs=4)
-                if part == 0:
-                    nc.scalar.activation(out=close[:], in_=root[:], func=ACT.Square)
-                else:
-                    nc.vector.tensor_tensor(close[:], root[:], root[:], ALU.mult)
-                nc.sync.dma_start(
-                    out_rows[:, 2 * pair : 2 * pair + 2, HALF * part : HALF * (part + 1)],
-                    close[:].rearrange("p (t m) -> p t m", t=2),
-                )
+        close = {}
+
+        def square(part, k, on_scalar):
+            close[part, k] = tile([P, BANK], F32, "close%d_%d" % (part, k))
+            t = close[part, k][:]
+            if on_scalar:
+                nc.scalar.activation(out=t, in_=y_acc[part, k][:], func=ACT.Square)
+            else:
+                nc.vector.tensor_copy(t, y_acc[part, k][:])
+                nc.vector.tensor_tensor(t, y_acc[part, k][:], t, ALU.mult)
+
+        def inverse_root(part, k):
+            t = close[part, k][:]
+            nc.scalar.activation(out=t, in_=t, func=ACT.Abs_reciprocal_sqrt, bias=1.0)
+
+        def store(part, k, on_scalar):
+            lo, width = PARTS[part]
+            per_bank = BANK // width
+            t = close[part, k][:]
+            if on_scalar:
+                nc.scalar.activation(out=t, in_=t, func=ACT.Square)
+            else:
+                nc.vector.tensor_tensor(t, t, t, ALU.mult)
+            nc.sync.dma_start(
+                out_rows[:, per_bank * k : per_bank * (k + 1), lo : lo + width],
+                t.rearrange("p (t m) -> p t m", t=per_bank),
+            )
 
         deal_w2(0)
         make_g(0)
-        pick_whole(0)
-        deal_w2_scales(1)
         make_w1(0, 0)
-        make_g(1)
-        pick_whole(1)
         make_w1(0, 1)
-        load_w3(0)
+        deal_w2(1)
+        make_w1(1, 0)
+        for s in range(1, 4):
+            make_g(s)
+        make_w1(1, 1)
         load_corr(4)
-        load_w3(1)
         load_corr(5)
         load_corr(6)
         load_corr(7)
-        make_g(2)
-        pick_whole(2)
-        deal_w2(1)
-        make_w1(1, 0)
-        for s in range(4):
+        load_w3(0)
+        load_w3(1)
+        for s in range(8):
             make_h(s)
             look(s)
-        make_w1(1, 1)
-        make_g(3)
-        pick_whole(3)
-        z_first = tile([P, PACK, HALF], BF16, "z_first")
-        for s in range(4):
-            limit(s, 0, z_first)
-        for s in range(4, 8):
-            make_h(s)
-            look(s)
-        make_w3(0)
-        make_z(0, 0, z_first[:])
-        make_w3(1)
-        multiply(0, 0)
-        left = tile([P, PACK, HALF], F32, "left", tag="picked_half")
-        z_left = tile([P, PACK, HALF], BF16, "z_left", tag="z_late")
         for s in range(4, 8):
             make_g(s)
-            pick_half(s, 0, left)
-            limit(s, 0, z_left)
-        make_z(1, 0, z_left[:])
-        multiply(1, 0)
-        right = tile([P, PACK, HALF], F32, "right", tag="picked_half")
-        for s in range(4, 8):
-            pick_half(s, 1, right)
-        z_right = tile([P, 2, PACK, HALF], BF16, "z_right", tag="z_late")
+        picked_low = tile([P, PACK, M], F32, "picked_low")
+        z_low = tile([P, PACK, M], BF16, "z_low")
+        for s in range(PACK):
+            pick(s, 0, picked_low[:, s])
+        for s in range(PACK):
+            limit(s, 0, picked_low[:, s], z_low[:, s])
         for b in range(2):
-            for s in range(PACK * b, PACK * (b + 1)):
-                limit(s, 1, z_right[:, b])
-            make_z(b, 1, z_right[:, b])
-        finish(0)
-        for b in range(2):
-            multiply(b, 1)
-        finish(1)
+            round_w3(b)
+            w3_q[b] = quantize(w3_bf[b][:], "w3_q%d" % b)
+        low_bf = tile([P, PACK * M], BF16, "low_bf")
+        weave(low_bf[:], z_low[:], True)
+        low_codes, low_scales = quantize(low_bf[:], "z_low_q")
+        for part, (lo, width) in enumerate(PARTS):
+            multiply(0, part, low_codes[:, lo : lo + width], low_scales[:, lo : lo + width])
+        for part, (lo, width) in enumerate(PARTS):
+            picked = tile([P, PACK, width], F32, "picked%d" % part, tag="picked_high")
+            z_high = tile([P, PACK, width], BF16, "z_high%d" % part)
+            high_bf = tile([P, PACK * width], BF16, "high_bf%d" % part)
+            for i in range(PACK):
+                pick(PACK + i, lo, picked[:, i])
+            for i in range(PACK):
+                limit(PACK + i, lo, picked[:, i], z_high[:, i])
+            weave(high_bf[:], z_high[:], part in (0,))
+            codes, scales = quantize(high_bf[:], "z_high_q%d" % part)
+            multiply(1, part, codes[:], scales[:])
+        for part, k in y_acc:
+            square(part, k, (part, k) not in ())
+            inverse_root(part, k)
+        for part, k in y_acc:
+            store(part, k, (part, k) in ())

@@ -19,12 +19,12 @@ ACT = mybir.ActivationFunctionType
 P = 128
 PACK = 4
 PASS = P * PACK
+QUADRANT = 32
 BANK = 512
 LIST = 16
+SLICES = H // P
+BANKS_EACH = 4
 PARTS = ((0, 128), (128, 256), (384, 128))
-CLEAR = 5120
-BANKS = {"g": 4, "h": 4}
-SHARED = ()
 
 
 def tile_list_stone_composition_closeness_kernel(
@@ -39,13 +39,13 @@ def tile_list_stone_composition_closeness_kernel(
             return sb.tile(shape, dtype, name=name, tag=tag or name, bufs=bufs, align_bytes=64)
 
         def bank(name, tag):
-            return ps.tile([P, BANK], F32, name=name, tag=tag, bufs=BANKS[tag])
+            return ps.tile([P, BANK], F32, name=name, tag=tag, bufs=BANKS_EACH)
 
-        tab_s = tile([P, 2 * T], U8, "tab_s")
-        nc.vector.memset(tab_s[:, :CLEAR].bitcast(I32), 0)
-        nc.gpsimd.memset(tab_s[:, CLEAR:].bitcast(I32), 0)
-        w2s_raw = tile([P, 2 * H], U8, "w2s_raw")
-        nc.vector.memset(w2s_raw[:].bitcast(I32), 0)
+        tab_s = [tile([P, T], U8, "tab_s%d" % a) for a in range(2)]
+        nc.vector.memset(tab_s[0][:].bitcast(I32), 0)
+        nc.gpsimd.memset(tab_s[1][:].bitcast(I32), 0)
+        w2_s_raw = tile([P, 2 * H], U8, "w2_s_raw")
+        nc.vector.memset(w2_s_raw[:].bitcast(I32), 0)
 
         offs_t = tile([P, S // LIST], U16, "offs_t")
         nc.sync.dma_start(offs_t[:], offs)
@@ -53,104 +53,105 @@ def tile_list_stone_composition_closeness_kernel(
         pos2_t = tile([P, M // LIST], U16, "pos2_t")
         nc.sync.dma_start(pos1_t[:], pos1)
         nc.sync.dma_start(pos2_t[:], pos2)
+
         tab_w = [tile([P, T], I32, "tab_w%d" % a) for a in range(2)]
 
-        def load_tab(a):
+        def load_tab_words(a):
             nc.sync.dma_start(tab_w[a][:], tab_words[a].rearrange("p t i -> p (t i)").bitcast(I32))
 
-        def load_scale_rows(plane, scales):
-            rows = scales.rearrange("a (q r) c -> r q a c", r=4)
-            for r in range(4):
-                nc.sync.dma_start(
-                    plane[r:P:32, :].rearrange("q (a c) -> q a c", a=2).bitcast(I32), rows[r].bitcast(I32)
-                )
+        def load_tab_scales(a):
+            rows = tab_scales[a].rearrange("(quad row) t -> row quad t", row=4)
+            for row in range(4):
+                nc.sync.dma_start(tab_s[a][row:P:QUADRANT, :].bitcast(I32), rows[row].bitcast(I32))
 
-        w2_raw = [tile([P, 2, PASS], U16, "w2_raw%d" % b) for b in range(2)]
+        def load_w2_scales():
+            rows = w2_scales.rearrange("a (quad row) c -> row quad a c", row=4)
+            for row in range(4):
+                into = w2_s_raw[row:P:QUADRANT, :].rearrange("quad (a c) -> quad a c", a=2)
+                nc.sync.dma_start(into.bitcast(I32), rows[row].bitcast(I32))
 
-        def load_w2(b):
+        w2_w_raw = [tile([P, 2, PASS], U16, "w2_w_raw%d" % b) for b in range(2)]
+
+        def load_w2_words(b):
             nc.sync.dma_start(
-                w2_raw[b][:].bitcast(I32),
+                w2_w_raw[b][:].bitcast(I32),
                 w2_words[:, :, 2 * PASS * b : 2 * PASS * (b + 1)].rearrange("a p c -> p a c").bitcast(I32),
             )
 
-        g = [tile([P, S], F32, "g%d" % s) for s in range(8)]
+        g = [tile([P, S], F32, "g%d" % s) for s in range(SLICES)]
         corr_rows = corr.rearrange("(b p i) j -> b i p j", b=2, i=PACK)
 
         def load_corr(s):
             nc.sync.dma_start(g[s][:], corr_rows[s // PACK, s % PACK])
 
-        w_raw = {}
+        w1_raw, w3_raw = {}, {}
 
         def load_w1(b, a):
-            w_raw[b, a] = tile([P, PACK, PASS], F32, "w1_raw%d%d" % (b, a), tag="w_raw", bufs=4)
+            w1_raw[b, a] = tile([P, PACK, PASS], F32, "w1_raw%d%d" % (b, a), tag="w_raw", bufs=4)
             rows = w1[PASS * a : PASS * (a + 1), PASS * b : PASS * (b + 1)]
-            nc.sync.dma_start(w_raw[b, a][:], rows.rearrange("(p j) c -> p j c", j=PACK))
-
-        w3_raw = {}
+            nc.sync.dma_start(w1_raw[b, a][:], rows.rearrange("(p j) c -> p j c", j=PACK))
 
         def load_w3(b):
             w3_raw[b] = tile([P, PACK, N], F32, "w3_raw%d" % b, tag="w_raw", bufs=4)
             nc.sync.dma_start(w3_raw[b][:], w3[PASS * b : PASS * (b + 1), :].rearrange("(p j) n -> p j n", j=PACK))
 
-        def load_rows(vec, name):
-            t = tile([P, 2, PACK], F32, name)
-            nc.sync.dma_start(t[:], vec.rearrange("(b p i) -> p b i", b=2, i=PACK))
-            return t[:].rearrange("p b i -> p (b i)")
+        def load_per_row(vec, name):
+            per_row = tile([P, 2, PACK], F32, name)
+            nc.sync.dma_start(per_row[:], vec.rearrange("(b p i) -> p b i", b=2, i=PACK))
+            return per_row[:].rearrange("p b i -> p (b i)")
 
-        load_w2(0)
-        load_scale_rows(tab_s, tab_scales)
-        load_tab(0)
-        load_scale_rows(w2s_raw, w2_scales)
-        load_tab(1)
+        load_w2_words(0)
+        load_tab_scales(0)
+        load_tab_scales(1)
+        load_w2_scales()
+        load_tab_words(0)
+        load_tab_words(1)
         load_corr(0)
         load_w1(0, 0)
         load_corr(1)
         load_w1(0, 1)
         load_corr(2)
-        slope_t = load_rows(slope, "slope_t")
-        share_t = load_rows(share, "share_t")
-        load_w2(1)
+        slope_t = load_per_row(slope, "slope_t")
+        share_t = load_per_row(share, "share_t")
+        load_w2_words(1)
         load_w1(1, 0)
         load_w1(1, 1)
         load_corr(3)
-        gain_t = load_rows(gain, "gain_t")
+        gain_t = load_per_row(gain, "gain_t")
 
         v_w = {}
 
         def gather_words(a):
             for u in range(2):
                 v_w[a, u] = tile([P, BANK], U32, "v_w%d%d" % (a, u))
-                cols = slice(u * BANK // LIST, (u + 1) * BANK // LIST)
-                nc.vector.tensor_copy(v_w[a, u][:], tab_w[a][:].bitcast(U32).indirect(offs_t[:, cols]))
+                entries = slice(u * BANK // LIST, (u + 1) * BANK // LIST)
+                nc.vector.tensor_copy(v_w[a, u][:], tab_w[a][:].bitcast(U32).indirect(offs_t[:, entries]))
 
-        w2_s = {}
+        w2_s, w2_w = {}, {}
 
         def deal_w2_scales(b):
             w2_s[b] = tile([P, 2, PASS], U8, "w2_s%d" % b)
             nc.vector.tensor_copy(
                 w2_s[b][:].rearrange("p a (i m) -> p a i m", i=PACK),
-                w2s_raw[:].rearrange("p (a b m i) -> p b a i m", a=2, b=2, i=PACK)[:, b],
+                w2_s_raw[:].rearrange("p (a b m i) -> p b a i m", a=2, b=2, i=PACK)[:, b],
+            )
+
+        def deal_w2_words(b):
+            w2_w[b] = tile([P, 2, PASS], U16, "w2_w%d" % b)
+            nc.scalar.copy(
+                w2_w[b][:].rearrange("p a (i m) -> p a i m", i=PACK),
+                w2_w_raw[b][:].rearrange("p a (m i) -> p a i m", i=PACK),
             )
 
         v_s = [tile([P, S], U8, "v_s%d" % a) for a in range(2)]
         for a in range(2):
-            nc.vector.tensor_copy(v_s[a][:], tab_s[:, T * a : T * (a + 1)].indirect(offs_t[:]))
-        gather_words(0)
-        deal_w2_scales(0)
-        gather_words(1)
-        deal_w2_scales(1)
+            nc.vector.tensor_copy(v_s[a][:], tab_s[a][:].indirect(offs_t[:]))
+        for half in range(2):
+            gather_words(half)
+            deal_w2_scales(half)
 
-        neg_ss = tile([P, 8], F32, "neg_ss")
-        nc.vector.scalar_tensor_tensor(neg_ss[:], slope_t, -1.0, share_t, ALU.mult, ALU.mult)
-
-        w2_w = {}
-
-        def deal_w2(b):
-            w2_w[b] = tile([P, 2, PASS], U16, "w2_w%d" % b)
-            nc.scalar.copy(
-                w2_w[b][:].rearrange("p a (i m) -> p a i m", i=PACK),
-                w2_raw[b][:].rearrange("p a (m i) -> p a i m", i=PACK),
-            )
+        neg_slope_share = tile([P, SLICES], F32, "neg_slope_share")
+        nc.vector.scalar_tensor_tensor(neg_slope_share[:], slope_t, -1.0, share_t, ALU.mult, ALU.mult)
 
         def quantize(grouped, name):
             width = grouped.shape[1] // PACK
@@ -162,199 +163,176 @@ def tile_list_stone_composition_closeness_kernel(
         w1_q = {}
 
         def make_w1(b, a):
-            name = "w1_bf%d%d" % (b, a)
-            grouped = tile([P, PASS * PACK], BF16, name, tag="w_bf", bufs=2)
+            grouped = tile([P, PASS * PACK], BF16, "w1_bf%d%d" % (b, a), tag="w1_bf", bufs=2)
             dst = grouped[:].rearrange("p (u e m j) -> p u m j e", u=2, e=2, j=PACK)
-            src = w_raw[b, a][:].rearrange("p j (m u e) -> p u m j e", u=2, e=2)
+            src = w1_raw[b, a][:].rearrange("p j (m u e) -> p u m j e", u=2, e=2)
             for u in range(2):
                 nc.scalar.copy(dst[:, u], src[:, u])
             w1_q[b, a] = quantize(grouped[:], "w1_q%d%d" % (b, a))
 
-        w3_bf, w3_q = {}, {}
+        def round_w3():
+            grouped = tile([P, 2 * N * PACK], BF16, "w3_bf", tag="h_last")
+            dst = grouped[:].rearrange("p (b u c e j) -> p b u c j e", b=2, u=2, e=PACK, j=PACK)
+            for b in range(2):
+                src = w3_raw[b][:].rearrange("p j (u c e) -> p u c j e", u=2, e=PACK)
+                for u in range(2):
+                    nc.scalar.copy(dst[:, b, u], src[:, u])
+            return grouped
 
-        def round_w3(b):
-            w3_bf[b] = tile([P, N * PACK], BF16, "w3_bf%d" % b, tag="w_bf", bufs=2)
-            dst = w3_bf[b][:].rearrange("p (u c e j) -> p u c j e", u=2, e=PACK, j=PACK)
-            src = w3_raw[b][:].rearrange("p j (u c e) -> p u c j e", u=2, e=PACK)
-            for u in range(2):
-                nc.scalar.copy(dst[:, u], src[:, u])
+        def times_table(acc, u, codes, scales):
+            for a in range(2):
+                nc.tensor.matmul_mx(
+                    out=acc[:],
+                    lhsT=codes[a],
+                    lhsT_scale=scales[a],
+                    rhs=v_w[a, u][:].bitcast(FP8X4),
+                    rhs_scale=v_s[a][:, u * BANK : (u + 1) * BANK],
+                    start=(a == 0),
+                    stop=(a == 1),
+                )
 
         def make_g(s):
             b, i = divmod(s, PACK)
+            places = slice(P * i, P * (i + 1))
+            codes = [w2_w[b][:, a, places].bitcast(FP4X4) for a in range(2)]
+            scales = [w2_s[b][:, a, places] for a in range(2)]
             for u in range(2):
                 cols = slice(u * BANK, (u + 1) * BANK)
                 acc = bank("g_acc%d%d" % (s, u), "g")
-                for a in range(2):
-                    nc.tensor.matmul_mx(
-                        out=acc[:],
-                        lhsT=w2_w[b][:, a, P * i : P * (i + 1)].bitcast(FP4X4),
-                        lhsT_scale=w2_s[b][:, a, P * i : P * (i + 1)],
-                        rhs=v_w[a, u][:].bitcast(FP8X4),
-                        rhs_scale=v_s[a][:, cols],
-                        start=(a == 0),
-                        stop=(a == 1),
-                    )
-                if s in SHARED:
-                    sums = tile([P, BANK], F32, "sums%d%d" % (s, u), tag="sums", bufs=3)
-                    nc.scalar.copy(sums[:], acc[:])
-                    nc.gpsimd.tensor_tensor(g[s][:, cols], sums[:], g[s][:, cols], ALU.add)
-                else:
-                    nc.vector.tensor_tensor(g[s][:, cols], acc[:], g[s][:, cols], ALU.add)
+                times_table(acc, u, codes, scales)
+                nc.vector.tensor_tensor(g[s][:, cols], acc[:], g[s][:, cols], ALU.add)
 
         h, bias = {}, {}
 
         def make_h(s):
             b, i = divmod(s, PACK)
-            h[s] = tile([P, S], F32, "h%d" % s, tag="h", bufs=4)
+            places = slice(P * i, P * (i + 1))
+            codes = [w1_q[b, a][0][:, places].bitcast(FP8X4) for a in range(2)]
+            scales = [w1_q[b, a][1][:, places] for a in range(2)]
+            if s == SLICES - 1:
+                h[s] = tile([P, S], F32, "h%d" % s, tag="h_last")
+            else:
+                h[s] = tile([P, S], F32, "h%d" % s, tag="h", bufs=4)
             tops = tile([P, 2], F32, "tops%d" % s)
             for u in range(2):
-                cols = slice(u * BANK, (u + 1) * BANK)
                 acc = bank("h_acc%d%d" % (s, u), "h")
-                for a in range(2):
-                    codes, scales = w1_q[b, a]
-                    nc.tensor.matmul_mx(
-                        out=acc[:],
-                        lhsT=codes[:, P * i : P * (i + 1)].bitcast(FP8X4),
-                        lhsT_scale=scales[:, P * i : P * (i + 1)],
-                        rhs=v_w[a, u][:].bitcast(FP8X4),
-                        rhs_scale=v_s[a][:, cols],
-                        start=(a == 0),
-                        stop=(a == 1),
-                    )
+                times_table(acc, u, codes, scales)
                 nc.vector.tensor_scalar(
-                    h[s][:, cols], acc[:], 1.0, None, ALU.mult, ALU.max, accum_out=tops[:, u : u + 1]
+                    h[s][:, u * BANK : (u + 1) * BANK], acc[:], 1.0, None, ALU.mult, ALU.max,
+                    accum_out=tops[:, u : u + 1],
                 )
-            bias[s] = tile([P, 8], F32, "bias%d" % s)
+            bias[s] = tile([P, 1], F32, "bias%d" % s)
             nc.gpsimd.tensor_scalar(
-                bias[s][:, 0:1], tops[:, 0:1], tops[:, 1:2], neg_ss[:, s : s + 1], ALU.max, ALU.mult
+                bias[s][:], tops[:, 0:1], tops[:, 1:2], neg_slope_share[:, s : s + 1], ALU.max, ALU.mult
             )
 
-        gate = {}
+        gate = [tile([P, PACK, M], F32, "gate%d" % b) for b in range(2)]
 
         def look(s):
-            gate[s] = tile([P, M], F32, "gate%d" % s)
             nc.scalar.activation(
-                out=gate[s][:],
+                out=gate[s // PACK][:, s % PACK],
                 in_=h[s][:].indirect(pos1_t[:]),
                 func=ACT.Sigmoid,
-                bias=bias[s][:, 0:1],
+                bias=bias[s][:],
                 scale=slope_t[:, s : s + 1],
             )
 
+        def amplify(s):
+            row = gate[s // PACK][:, s % PACK]
+            nc.gpsimd.tensor_scalar(row, row, gain_t[:, s : s + 1], 0.0, ALU.mult, ALU.add)
+
         def pick(s, lo, into):
-            cols = slice(lo // LIST, (lo + into.shape[1]) // LIST)
-            nc.vector.tensor_copy(into, g[s][:].indirect(pos2_t[:, cols]))
+            entries = slice(lo // LIST, (lo + into.shape[1]) // LIST)
+            nc.vector.tensor_copy(into, g[s][:].indirect(pos2_t[:, entries]))
 
-        def limit(s, lo, picked, z_row):
-            width = picked.shape[1]
-            nc.vector.scalar_tensor_tensor(
-                z_row, gate[s][:, lo : lo + width], gain_t[:, s : s + 1], picked, ALU.mult, ALU.min
+        def limit(b, lo, picked, grouped):
+            width = picked.shape[2]
+            nc.vector.tensor_tensor(
+                grouped.rearrange("p (c e j) -> p c j e", e=2, j=PACK),
+                picked.rearrange("p j (c e) -> p c j e", e=2),
+                gate[b][:, :, lo : lo + width].rearrange("p j (c e) -> p c j e", e=2),
+                ALU.min,
             )
-
-        def weave(grouped, z_rows, on_scalar):
-            dst = grouped.rearrange("p (c e j) -> p c j e", e=PACK, j=PACK)
-            src = z_rows.rearrange("p j (c e) -> p c j e", e=PACK)
-            if on_scalar:
-                nc.scalar.copy(dst, src)
-            else:
-                nc.vector.tensor_copy(dst, src)
 
         out_rows = out.rearrange("(t p) m -> p t m", p=P)
         y_acc = {}
 
-        def multiply(b, part, z_codes, z_scales):
+        def make_y(part, z_q):
             width = PARTS[part][1]
             per_bank = BANK // width
-            w_codes, w_scales = w3_q[b]
-            for t in range(N // P):
-                k, dt = divmod(t, per_bank)
-                if b == 0 and dt == 0:
-                    y_acc[part, k] = bank("y_acc%d_%d" % (part, k), "h")
-                nc.tensor.matmul_mx(
-                    out=y_acc[part, k][:, dt * width : (dt + 1) * width],
-                    lhsT=w_codes[:, P * t : P * (t + 1)].bitcast(FP8X4),
-                    lhsT_scale=w_scales[:, P * t : P * (t + 1)],
-                    rhs=z_codes.bitcast(FP8X4),
-                    rhs_scale=z_scales,
-                    start=(b == 0 and dt == 0),
-                    stop=(b == 1 and dt == per_bank - 1),
-                )
+            for nth in range(N // P // per_bank):
+                y_acc[part, nth] = bank("y_acc%d_%d" % (part, nth), "h")
+                for b in range(2):
+                    z_codes, z_scales = z_q[b]
+                    for place in range(per_bank):
+                        t = per_bank * nth + place
+                        cols = slice(N * b + P * t, N * b + P * (t + 1))
+                        nc.tensor.matmul_mx(
+                            out=y_acc[part, nth][:, place * width : (place + 1) * width],
+                            lhsT=w3_codes[:, cols].bitcast(FP8X4),
+                            lhsT_scale=w3_scales[:, cols],
+                            rhs=z_codes[:].bitcast(FP8X4),
+                            rhs_scale=z_scales[:],
+                            start=(b == 0 and place == 0),
+                            stop=(b == 1 and place == per_bank - 1),
+                        )
 
-        close = {}
-
-        def square(part, k, on_scalar):
-            close[part, k] = tile([P, BANK], F32, "close%d_%d" % (part, k))
-            t = close[part, k][:]
-            if on_scalar:
-                nc.scalar.activation(out=t, in_=y_acc[part, k][:], func=ACT.Square)
-            else:
-                nc.vector.tensor_copy(t, y_acc[part, k][:])
-                nc.vector.tensor_tensor(t, y_acc[part, k][:], t, ALU.mult)
-
-        def inverse_root(part, k):
-            t = close[part, k][:]
-            nc.scalar.activation(out=t, in_=t, func=ACT.Abs_reciprocal_sqrt, bias=1.0)
-
-        def store(part, k, on_scalar):
+        def inverse_roots(part, step):
             lo, width = PARTS[part]
-            per_bank = BANK // width
-            t = close[part, k][:]
-            if on_scalar:
-                nc.scalar.activation(out=t, in_=t, func=ACT.Square)
-            else:
-                nc.vector.tensor_tensor(t, t, t, ALU.mult)
-            nc.sync.dma_start(
-                out_rows[:, per_bank * k : per_bank * (k + 1), lo : lo + width],
-                t.rearrange("p (t m) -> p t m", t=per_bank),
-            )
+            pieces = []
+            for t in range(0, N // P, step):
+                nth, place = divmod(t, BANK // width)
+                piece = tile([P, step * width], F32, "close%d_%d" % (part, t))
+                sums = y_acc[part, nth][:, place * width : (place + step) * width]
+                nc.scalar.activation(out=piece[:], in_=sums, func=ACT.Square)
+                pieces.append((piece[:], out_rows[:, t : t + step, lo : lo + width]))
+            for piece, rows in pieces:
+                nc.scalar.activation(out=piece, in_=piece, func=ACT.Abs_reciprocal_sqrt, bias=1.0)
+            return pieces
 
-        deal_w2(0)
+        def store(piece, rows):
+            nc.sync.dma_start(rows, piece.rearrange("p (t m) -> p t m", t=rows.shape[1]))
+
+        deal_w2_words(0)
         make_g(0)
         make_w1(0, 0)
         make_w1(0, 1)
-        deal_w2(1)
+        deal_w2_words(1)
         make_w1(1, 0)
-        for s in range(1, 4):
+        for s in range(1, PACK):
             make_g(s)
         make_w1(1, 1)
-        load_corr(4)
-        load_corr(5)
-        load_corr(6)
-        load_corr(7)
-        load_w3(0)
-        load_w3(1)
-        for s in range(8):
+        for s in range(PACK, SLICES):
+            load_corr(s)
+        for b in range(2):
+            load_w3(b)
+        for s in range(SLICES):
             make_h(s)
             look(s)
-        for s in range(4, 8):
+        for s in range(SLICES):
+            amplify(s)
+        for s in range(PACK, SLICES):
             make_g(s)
         picked_low = tile([P, PACK, M], F32, "picked_low")
-        z_low = tile([P, PACK, M], BF16, "z_low")
         for s in range(PACK):
             pick(s, 0, picked_low[:, s])
-        for s in range(PACK):
-            limit(s, 0, picked_low[:, s], z_low[:, s])
-        for b in range(2):
-            round_w3(b)
-            w3_q[b] = quantize(w3_bf[b][:], "w3_q%d" % b)
-        low_bf = tile([P, PACK * M], BF16, "low_bf")
-        weave(low_bf[:], z_low[:], True)
-        low_codes, low_scales = quantize(low_bf[:], "z_low_q")
+        w3_bf = round_w3()
+
         for part, (lo, width) in enumerate(PARTS):
-            multiply(0, part, low_codes[:, lo : lo + width], low_scales[:, lo : lo + width])
-        for part, (lo, width) in enumerate(PARTS):
-            picked = tile([P, PACK, width], F32, "picked%d" % part, tag="picked_high")
-            z_high = tile([P, PACK, width], BF16, "z_high%d" % part)
-            high_bf = tile([P, PACK * width], BF16, "high_bf%d" % part)
+            picked_high = tile([P, PACK, width], F32, "picked_high%d" % part, tag="picked_high")
             for i in range(PACK):
-                pick(PACK + i, lo, picked[:, i])
-            for i in range(PACK):
-                limit(PACK + i, lo, picked[:, i], z_high[:, i])
-            weave(high_bf[:], z_high[:], part in (0,))
-            codes, scales = quantize(high_bf[:], "z_high_q%d" % part)
-            multiply(1, part, codes[:], scales[:])
-        for part, k in y_acc:
-            square(part, k, (part, k) not in ())
-            inverse_root(part, k)
-        for part, k in y_acc:
-            store(part, k, (part, k) in ())
+                pick(PACK + i, lo, picked_high[:, i])
+            z_bf = [tile([P, PACK * width], BF16, "z_bf%d_%d" % (b, part), tag="z_bf", bufs=2) for b in range(2)]
+            limit(0, lo, picked_low[:, :, lo : lo + width], z_bf[0][:])
+            limit(1, lo, picked_high[:], z_bf[1][:])
+            if part == 0:
+                w3_codes, w3_scales = quantize(w3_bf[:], "w3_q")
+            make_y(part, [quantize(z_bf[b][:], "z_q%d_%d" % (b, part)) for b in range(2)])
+
+        for piece, rows in inverse_roots(0, N // P):
+            nc.scalar.activation(out=piece, in_=piece, func=ACT.Square)
+            store(piece, rows)
+        later = [found for part in range(1, len(PARTS)) for found in inverse_roots(part, N // P // 2)]
+        for piece, rows in later:
+            nc.vector.tensor_tensor(piece, piece, piece, ALU.mult)
+            store(piece, rows)

from contextlib import ExitStack

import concourse.mybir as mybir

K, T, S, M, H, N = 1024, 4096, 1024, 512, 1024, 512
FLOPS = 2 * (2 * K * H * S + H * N * M)

F32 = mybir.dt.float32
BF16 = mybir.dt.bfloat16
I32 = mybir.dt.int32
U32 = mybir.dt.uint32
U16 = mybir.dt.uint16
U8 = mybir.dt.uint8
FP8X4 = mybir.dt.float8_e4m3fn_x4
FP4X4 = mybir.dt.float4_e2m1fn_x4
ALU = mybir.AluOpType
ACT = mybir.ActivationFunctionType

P = 128
PACK = 4
PASS = P * PACK
QUADRANT = 32
BANK = 512
LIST = 16
SLICES = H // P
BANKS_EACH = 4
PARTS = ((0, 128), (128, 256), (384, 128))


def tile_list_stone_composition_closeness_kernel(
    tc, tab_words, tab_scales, offs, pos1, pos2, w1, w2_words, w2_scales, corr, slope, share, gain, w3, out
):
    nc = tc.nc
    with ExitStack() as ctx:
        sb = ctx.enter_context(tc.tile_pool(name="sb", bufs=1))
        ps = ctx.enter_context(tc.psum_pool(name="ps", bufs=1))

        def tile(shape, dtype, name, tag=None, bufs=1):
            return sb.tile(shape, dtype, name=name, tag=tag or name, bufs=bufs, align_bytes=64)

        def bank(name, tag):
            return ps.tile([P, BANK], F32, name=name, tag=tag, bufs=BANKS_EACH)

        tab_s = [tile([P, T], U8, "tab_s%d" % a) for a in range(2)]
        nc.vector.memset(tab_s[0][:].bitcast(I32), 0)
        nc.gpsimd.memset(tab_s[1][:].bitcast(I32), 0)
        w2_s_raw = tile([P, 2 * H], U8, "w2_s_raw")
        nc.vector.memset(w2_s_raw[:].bitcast(I32), 0)

        offs_t = tile([P, S // LIST], U16, "offs_t")
        nc.sync.dma_start(offs_t[:], offs)
        pos1_t = tile([P, M // LIST], U16, "pos1_t")
        pos2_t = tile([P, M // LIST], U16, "pos2_t")
        nc.sync.dma_start(pos1_t[:], pos1)
        nc.sync.dma_start(pos2_t[:], pos2)

        tab_w = [tile([P, T], I32, "tab_w%d" % a) for a in range(2)]

        def load_tab_words(a):
            nc.sync.dma_start(tab_w[a][:], tab_words[a].rearrange("p t i -> p (t i)").bitcast(I32))

        def load_tab_scales(a):
            rows = tab_scales[a].rearrange("(quad row) t -> row quad t", row=4)
            for row in range(4):
                nc.sync.dma_start(tab_s[a][row:P:QUADRANT, :].bitcast(I32), rows[row].bitcast(I32))

        def load_w2_scales():
            rows = w2_scales.rearrange("a (quad row) c -> row quad a c", row=4)
            for row in range(4):
                into = w2_s_raw[row:P:QUADRANT, :].rearrange("quad (a c) -> quad a c", a=2)
                nc.sync.dma_start(into.bitcast(I32), rows[row].bitcast(I32))

        w2_w_raw = [tile([P, 2, PASS], U16, "w2_w_raw%d" % b) for b in range(2)]

        def load_w2_words(b):
            nc.sync.dma_start(
                w2_w_raw[b][:].bitcast(I32),
                w2_words[:, :, 2 * PASS * b : 2 * PASS * (b + 1)].rearrange("a p c -> p a c").bitcast(I32),
            )

        g = [tile([P, S], F32, "g%d" % s) for s in range(SLICES)]
        corr_rows = corr.rearrange("(b p i) j -> b i p j", b=2, i=PACK)

        def load_corr(s):
            nc.sync.dma_start(g[s][:], corr_rows[s // PACK, s % PACK])

        w1_raw, w3_raw = {}, {}

        def load_w1(b, a):
            w1_raw[b, a] = tile([P, PACK, PASS], F32, "w1_raw%d%d" % (b, a), tag="w_raw", bufs=4)
            rows = w1[PASS * a : PASS * (a + 1), PASS * b : PASS * (b + 1)]
            nc.sync.dma_start(w1_raw[b, a][:], rows.rearrange("(p j) c -> p j c", j=PACK))

        def load_w3(b):
            w3_raw[b] = tile([P, PACK, N], F32, "w3_raw%d" % b, tag="w_raw", bufs=4)
            nc.sync.dma_start(w3_raw[b][:], w3[PASS * b : PASS * (b + 1), :].rearrange("(p j) n -> p j n", j=PACK))

        def load_per_row(vec, name):
            per_row = tile([P, 2, PACK], F32, name)
            nc.sync.dma_start(per_row[:], vec.rearrange("(b p i) -> p b i", b=2, i=PACK))
            return per_row[:].rearrange("p b i -> p (b i)")

        load_w2_words(0)
        load_tab_scales(0)
        load_tab_scales(1)
        load_w2_scales()
        load_tab_words(0)
        load_tab_words(1)
        load_corr(0)
        load_w1(0, 0)
        load_corr(1)
        load_w1(0, 1)
        load_corr(2)
        slope_t = load_per_row(slope, "slope_t")
        share_t = load_per_row(share, "share_t")
        load_w2_words(1)
        load_w1(1, 0)
        load_w1(1, 1)
        load_corr(3)
        gain_t = load_per_row(gain, "gain_t")

        v_w = {}

        def gather_words(a):
            for u in range(2):
                v_w[a, u] = tile([P, BANK], U32, "v_w%d%d" % (a, u))
                entries = slice(u * BANK // LIST, (u + 1) * BANK // LIST)
                nc.vector.tensor_copy(v_w[a, u][:], tab_w[a][:].bitcast(U32).indirect(offs_t[:, entries]))

        w2_s, w2_w = {}, {}

        def deal_w2_scales(b):
            w2_s[b] = tile([P, 2, PASS], U8, "w2_s%d" % b)
            nc.vector.tensor_copy(
                w2_s[b][:].rearrange("p a (i m) -> p a i m", i=PACK),
                w2_s_raw[:].rearrange("p (a b m i) -> p b a i m", a=2, b=2, i=PACK)[:, b],
            )

        def deal_w2_words(b):
            w2_w[b] = tile([P, 2, PASS], U16, "w2_w%d" % b)
            nc.scalar.copy(
                w2_w[b][:].rearrange("p a (i m) -> p a i m", i=PACK),
                w2_w_raw[b][:].rearrange("p a (m i) -> p a i m", i=PACK),
            )

        v_s = [tile([P, S], U8, "v_s%d" % a) for a in range(2)]
        for a in range(2):
            nc.vector.tensor_copy(v_s[a][:], tab_s[a][:].indirect(offs_t[:]))
        for half in range(2):
            gather_words(half)
            deal_w2_scales(half)

        neg_slope_share = tile([P, SLICES], F32, "neg_slope_share")
        nc.vector.scalar_tensor_tensor(neg_slope_share[:], slope_t, -1.0, share_t, ALU.mult, ALU.mult)

        def quantize(grouped, name):
            width = grouped.shape[1] // PACK
            codes = tile([P, width], U32, name + "_w")
            scales = tile([P, width], U8, name + "_s")
            nc.vector.quantize_mx(out=codes[:].bitcast(FP8X4), scales=scales[:], in_=grouped)
            return codes, scales

        w1_q = {}

        def make_w1(b, a):
            grouped = tile([P, PASS * PACK], BF16, "w1_bf%d%d" % (b, a), tag="w1_bf", bufs=2)
            dst = grouped[:].rearrange("p (u e m j) -> p u m j e", u=2, e=2, j=PACK)
            src = w1_raw[b, a][:].rearrange("p j (m u e) -> p u m j e", u=2, e=2)
            for u in range(2):
                nc.scalar.copy(dst[:, u], src[:, u])
            w1_q[b, a] = quantize(grouped[:], "w1_q%d%d" % (b, a))

        def round_w3():
            grouped = tile([P, 2 * N * PACK], BF16, "w3_bf", tag="h_last")
            dst = grouped[:].rearrange("p (b u c e j) -> p b u c j e", b=2, u=2, e=PACK, j=PACK)
            for b in range(2):
                src = w3_raw[b][:].rearrange("p j (u c e) -> p u c j e", u=2, e=PACK)
                for u in range(2):
                    nc.scalar.copy(dst[:, b, u], src[:, u])
            return grouped

        def times_table(acc, u, codes, scales):
            for a in range(2):
                nc.tensor.matmul_mx(
                    out=acc[:],
                    lhsT=codes[a],
                    lhsT_scale=scales[a],
                    rhs=v_w[a, u][:].bitcast(FP8X4),
                    rhs_scale=v_s[a][:, u * BANK : (u + 1) * BANK],
                    start=(a == 0),
                    stop=(a == 1),
                )

        def make_g(s):
            b, i = divmod(s, PACK)
            places = slice(P * i, P * (i + 1))
            codes = [w2_w[b][:, a, places].bitcast(FP4X4) for a in range(2)]
            scales = [w2_s[b][:, a, places] for a in range(2)]
            for u in range(2):
                cols = slice(u * BANK, (u + 1) * BANK)
                acc = bank("g_acc%d%d" % (s, u), "g")
                times_table(acc, u, codes, scales)
                nc.vector.tensor_tensor(g[s][:, cols], acc[:], g[s][:, cols], ALU.add)

        h, bias = {}, {}

        def make_h(s):
            b, i = divmod(s, PACK)
            places = slice(P * i, P * (i + 1))
            codes = [w1_q[b, a][0][:, places].bitcast(FP8X4) for a in range(2)]
            scales = [w1_q[b, a][1][:, places] for a in range(2)]
            if s == SLICES - 1:
                h[s] = tile([P, S], F32, "h%d" % s, tag="h_last")
            else:
                h[s] = tile([P, S], F32, "h%d" % s, tag="h", bufs=4)
            tops = tile([P, 2], F32, "tops%d" % s)
            for u in range(2):
                acc = bank("h_acc%d%d" % (s, u), "h")
                times_table(acc, u, codes, scales)
                nc.vector.tensor_scalar(
                    h[s][:, u * BANK : (u + 1) * BANK], acc[:], 1.0, None, ALU.mult, ALU.max,
                    accum_out=tops[:, u : u + 1],
                )
            bias[s] = tile([P, 1], F32, "bias%d" % s)
            nc.gpsimd.tensor_scalar(
                bias[s][:], tops[:, 0:1], tops[:, 1:2], neg_slope_share[:, s : s + 1], ALU.max, ALU.mult
            )

        gate = [tile([P, PACK, M], F32, "gate%d" % b) for b in range(2)]

        def look(s):
            nc.scalar.activation(
                out=gate[s // PACK][:, s % PACK],
                in_=h[s][:].indirect(pos1_t[:]),
                func=ACT.Sigmoid,
                bias=bias[s][:],
                scale=slope_t[:, s : s + 1],
            )

        def amplify(s):
            row = gate[s // PACK][:, s % PACK]
            nc.gpsimd.tensor_scalar(row, row, gain_t[:, s : s + 1], 0.0, ALU.mult, ALU.add)

        def pick(s, lo, into):
            entries = slice(lo // LIST, (lo + into.shape[1]) // LIST)
            nc.vector.tensor_copy(into, g[s][:].indirect(pos2_t[:, entries]))

        def limit(b, lo, picked, grouped):
            width = picked.shape[2]
            nc.vector.tensor_tensor(
                grouped.rearrange("p (c e j) -> p c j e", e=2, j=PACK),
                picked.rearrange("p j (c e) -> p c j e", e=2),
                gate[b][:, :, lo : lo + width].rearrange("p j (c e) -> p c j e", e=2),
                ALU.min,
            )

        out_rows = out.rearrange("(t p) m -> p t m", p=P)
        y_acc = {}

        def make_y(part, z_q):
            width = PARTS[part][1]
            per_bank = BANK // width
            for nth in range(N // P // per_bank):
                y_acc[part, nth] = bank("y_acc%d_%d" % (part, nth), "h")
                for b in range(2):
                    z_codes, z_scales = z_q[b]
                    for place in range(per_bank):
                        t = per_bank * nth + place
                        cols = slice(N * b + P * t, N * b + P * (t + 1))
                        nc.tensor.matmul_mx(
                            out=y_acc[part, nth][:, place * width : (place + 1) * width],
                            lhsT=w3_codes[:, cols].bitcast(FP8X4),
                            lhsT_scale=w3_scales[:, cols],
                            rhs=z_codes[:].bitcast(FP8X4),
                            rhs_scale=z_scales[:],
                            start=(b == 0 and place == 0),
                            stop=(b == 1 and place == per_bank - 1),
                        )

        def inverse_roots(part, step):
            lo, width = PARTS[part]
            pieces = []
            for t in range(0, N // P, step):
                nth, place = divmod(t, BANK // width)
                piece = tile([P, step * width], F32, "close%d_%d" % (part, t))
                sums = y_acc[part, nth][:, place * width : (place + step) * width]
                nc.scalar.activation(out=piece[:], in_=sums, func=ACT.Square)
                pieces.append((piece[:], out_rows[:, t : t + step, lo : lo + width]))
            for piece, rows in pieces:
                nc.scalar.activation(out=piece, in_=piece, func=ACT.Abs_reciprocal_sqrt, bias=1.0)
            return pieces

        def store(piece, rows):
            nc.sync.dma_start(rows, piece.rearrange("p (t m) -> p t m", t=rows.shape[1]))

        deal_w2_words(0)
        make_g(0)
        make_w1(0, 0)
        make_w1(0, 1)
        deal_w2_words(1)
        make_w1(1, 0)
        for s in range(1, PACK):
            make_g(s)
        make_w1(1, 1)
        for s in range(PACK, SLICES):
            load_corr(s)
        for b in range(2):
            load_w3(b)
        for s in range(SLICES):
            make_h(s)
            look(s)
        for s in range(SLICES):
            amplify(s)
        for s in range(PACK, SLICES):
            make_g(s)
        picked_low = tile([P, PACK, M], F32, "picked_low")
        for s in range(PACK):
            pick(s, 0, picked_low[:, s])
        w3_bf = round_w3()

        for part, (lo, width) in enumerate(PARTS):
            picked_high = tile([P, PACK, width], F32, "picked_high%d" % part, tag="picked_high")
            for i in range(PACK):
                pick(PACK + i, lo, picked_high[:, i])
            z_bf = [tile([P, PACK * width], BF16, "z_bf%d_%d" % (b, part), tag="z_bf", bufs=2) for b in range(2)]
            limit(0, lo, picked_low[:, :, lo : lo + width], z_bf[0][:])
            limit(1, lo, picked_high[:], z_bf[1][:])
            if part == 0:
                w3_codes, w3_scales = quantize(w3_bf[:], "w3_q")
            make_y(part, [quantize(z_bf[b][:], "z_q%d_%d" % (b, part)) for b in range(2)])

        for piece, rows in inverse_roots(0, N // P):
            nc.scalar.activation(out=piece, in_=piece, func=ACT.Square)
            store(piece, rows)
        later = [found for part in range(1, len(PARTS)) for found in inverse_roots(part, N // P // 2)]
        for piece, rows in later:
            nc.vector.tensor_tensor(piece, piece, piece, ALU.mult)
            store(piece, rows)
